import numpy as np
import ml_dtypes


def mxq(x, axis, fmt="e4m3"):
    dtype, down = {"e4m3": (ml_dtypes.float8_e4m3fn, 7), "e5m2": (ml_dtypes.float8_e5m2, 14)}[fmt]
    v = np.moveaxis(np.asarray(x, np.float32).astype(ml_dtypes.bfloat16).astype(np.float64), axis, -1)
    blocks = v.reshape(v.shape[:-1] + (-1, 32))
    amax = np.abs(blocks).max(-1, keepdims=True)
    byte = np.maximum(np.where(amax > 0, np.frexp(amax)[1] - 1 + 127, 0) - down, 1)
    scale = np.exp2(byte - 127.0)
    codes = (blocks / scale).astype(np.float32).astype(dtype).astype(np.float64)
    return np.moveaxis((codes * scale).reshape(v.shape), -1, axis)


WIDE = False


def mx_kscale(k):
    if not WIDE:
        return np.ones(k)
    levels = np.array([10, -10, 5, -5, 0])
    if k % 512:
        return np.exp2(np.random.permutation(np.resize(levels, k // 32))).repeat(32)
    a = np.empty((k // 512, 16))
    for p in range(k // 512):
        a[p, :8] = np.random.permutation(np.resize(levels, 8))
        for g in range(8):
            far = levels[np.abs(levels - a[p, g]) >= 10]
            a[p, g + 8] = far[np.random.randint(len(far))]
    return np.exp2(a.ravel()).repeat(32)


def f64(x):
    return np.asarray(x).astype(np.float64)


def striped(idx):
    return np.tile(idx.reshape(-1, 16).T, (8, 1)).astype(np.uint16)


def unstriped(offs):
    return offs[:16].T.reshape(-1).astype(np.int64)


def pack_weight(w):
    k, n = w.shape
    w = f64(np.asarray(w, np.float32).astype(ml_dtypes.bfloat16)).reshape(k // 32, 32, n)
    amax = np.abs(w).max(1)
    byte = np.clip(np.where(amax > 0, np.frexp(amax)[1] - 1 + 127 - 7, 1), 1, 254)
    scaled = (w * np.exp2(127.0 - byte)[:, None, :]).reshape(k, n).astype(np.float32)
    words = np.ascontiguousarray(scaled.reshape(k // 512, 128, 4, n).transpose(0, 1, 3, 2)).astype(ml_dtypes.float8_e4m3fn).view(np.uint8)
    return words, np.ascontiguousarray(byte.astype(np.uint8).reshape(k // 512, 16, n))


def unpack_weight(words, scales):
    g, p, n, _ = words.shape
    vals = np.ascontiguousarray(words).view(ml_dtypes.float8_e4m3fn).astype(np.float64) * np.repeat(np.exp2(scales.astype(np.float64) - 127.0), 8, axis=1)[..., None]
    return vals.transpose(0, 1, 3, 2).reshape(g * 512, n)


def relu(v):
    return np.maximum(v, 0.0)


K, T, S, V, N = 512, 4096, 1024, 512, 128


def setup_inputs():
    n = np.random.standard_normal
    s = mx_kscale(K)[:, None]
    packed_xT = pack_weight(n((K, T)) * s)
    return {
        "x_words": packed_xT[0],
        "x_scales": packed_xT[1],
        "sT": (n((K, V)) * s).astype(np.float32),
        "w1": (n((K, N)) / np.sqrt(K) / s).astype(np.float32),
        "w2": (n((K, N)) / np.sqrt(K) / s).astype(np.float32),
        "offs": striped(np.random.permutation(T)[:S]),
        "par": striped(np.random.randint(0, V, S)),
    }


def reference(x_words, x_scales, sT, w1, w2, offs, par):
    xq = unpack_weight(x_words, x_scales)[:, unstriped(offs)]
    y = mxq(f64(w1), 0, "e4m3").T @ xq
    t = mxq(f64(w2), 0, "e4m3").T @ mxq(f64(sT), 0, "e4m3")
    return relu(y + t[:, unstriped(par)])

@@ -1,0 +1,123 @@
+from contextlib import ExitStack
+
+import concourse.mybir as mybir
+
+K, T, S, V, N = 512, 4096, 1024, 512, 128
+FLOPS = 2 * K * N * (S + V)
+
+F32 = mybir.dt.float32
+BF16 = mybir.dt.bfloat16
+I32 = mybir.dt.int32
+U32 = mybir.dt.uint32
+U16 = mybir.dt.uint16
+U8 = mybir.dt.uint8
+FP8X4 = mybir.dt.float8_e4m3fn_x4
+ACT = mybir.ActivationFunctionType
+ALU = mybir.AluOpType
+
+P = 128
+PACK = 4
+PER_COL = 16
+HALF_S = S // 2
+HALF_V = V // 2
+PIECE = 256
+
+
+def weave_views(grouped, raw):
+    return (
+        grouped[:].rearrange("p (c i) j -> p c j i", i=4),
+        raw[:].rearrange("p j (c i) -> p c j i", i=4),
+    )
+
+
+def quantize(nc, codes, scales, grouped):
+    nc.vector.quantize_mx(out=codes.bitcast(FP8X4), scales=scales, in_=grouped[:].rearrange("p c j -> p (c j)"))
+
+
+def tile_picked_fpn_relu_p_kernel(tc, x_words, x_scales, sT, w1, w2, offs, par, out):
+    nc = tc.nc
+    with ExitStack() as ctx:
+        lists = ctx.enter_context(tc.tile_pool(name="lists", bufs=1))
+        held = ctx.enter_context(tc.tile_pool(name="held", bufs=1))
+        psum = ctx.enter_context(tc.psum_pool(name="psum", bufs=1))
+
+        offs_sb = lists.tile([P, S // PER_COL], U16, name="offs_sb")
+        par_sb = lists.tile([P, S // PER_COL], U16, name="par_sb")
+        xw = held.tile([P, T], I32, name="xw", align_bytes=64)
+        xs = held.tile([P, T], U8, name="xs", align_bytes=64)
+        w1_raw = held.tile([P, PACK, N], F32, name="w1_raw")
+        w2_raw = held.tile([P, PACK, N], F32, name="w2_raw")
+        s_raw = [held.tile([P, PACK, HALF_V], F32, name=f"s_raw{h}") for h in range(2)]
+
+        nc.vector.memset(xs[:].bitcast(I32), 0)
+        s_rows = sT.rearrange("(p j) v -> p j v", j=PACK)
+        nc.sync.dma_start(out=w2_raw[:], in_=w2.rearrange("(p j) n -> p j n", j=PACK))
+        nc.sync.dma_start(out=s_raw[0][:], in_=s_rows[:, :, 0:HALF_V])
+        nc.sync.dma_start(offs_sb[:], offs)
+        nc.sync.dma_start(out=s_raw[1][:], in_=s_rows[:, :, HALF_V:V])
+        for q in range(4):
+            nc.scalar.dma_start(
+                out=xs[32 * q : 32 * q + 4, :].bitcast(I32), in_=x_scales[0, 4 * q : 4 * q + 4, :].bitcast(I32)
+            )
+        nc.sync.dma_start(par_sb[:], par)
+        nc.sync.dma_start(out=w1_raw[:], in_=w1.rearrange("(p j) n -> p j n", j=PACK))
+        nc.sync.dma_start(out=xw[:], in_=x_words[0].rearrange("p c r -> p (c r)").bitcast(I32))
+
+        w1_bf = held.tile([P, N, PACK], BF16, name="w1_bf", align_bytes=64)
+        w2_bf = held.tile([P, N, PACK], BF16, name="w2_bf", align_bytes=64)
+        s_bf = [held.tile([P, HALF_V, PACK], BF16, name=f"s_bf{h}", align_bytes=64) for h in range(2)]
+        w1_codes = held.tile([P, N], U32, name="w1_codes", align_bytes=64)
+        w1_scales = held.tile([P, N], U8, name="w1_scales", align_bytes=64)
+        w2_codes = held.tile([P, N], U32, name="w2_codes", align_bytes=64)
+        w2_scales = held.tile([P, N], U8, name="w2_scales", align_bytes=64)
+        s_codes = [held.tile([P, HALF_V], U32, name=f"s_codes{h}", align_bytes=64) for h in range(2)]
+        s_scales = [held.tile([P, HALF_V], U8, name=f"s_scales{h}", align_bytes=64) for h in range(2)]
+        t_sb = held.tile([P, V], F32, name="t_sb", align_bytes=64)
+        kept_scales = held.tile([P, S], U8, name="kept_scales", align_bytes=64)
+        kept_words = [held.tile([P, HALF_S], U32, name=f"kept_words{h}", align_bytes=64) for h in range(2)]
+        parent = held.tile([P, S], F32, name="parent", align_bytes=64)
+        t_ps = [psum.tile([P, HALF_V], F32, name=f"t_ps{h}") for h in range(2)]
+        y_ps = [psum.tile([P, HALF_S], F32, name=f"y_ps{h}") for h in range(2)]
+
+        dst, src = weave_views(w2_bf, w2_raw)
+        nc.scalar.activation(out=dst, in_=src, func=ACT.Copy)
+        nc.vector.tensor_copy(kept_scales[:], xs[:].indirect(offs_sb[:]))
+        quantize(nc, w2_codes[:], w2_scales[:], w2_bf)
+        for h in range(2):
+            dst, src = weave_views(s_bf[h], s_raw[h])
+            nc.scalar.copy(out=dst, in_=src)
+            quantize(nc, s_codes[h][:], s_scales[h][:], s_bf[h])
+            nc.tensor.matmul_mx(
+                out=t_ps[h][:], lhsT=w2_codes[:].bitcast(FP8X4), lhsT_scale=w2_scales[:],
+                rhs=s_codes[h][:].bitcast(FP8X4), rhs_scale=s_scales[h][:], start=True, stop=True,
+            )
+        for h in range(2):
+            nc.scalar.copy(out=t_sb[:, h * HALF_V : (h + 1) * HALF_V], in_=t_ps[h][:])
+        dst, src = weave_views(w1_bf, w1_raw)
+        nc.scalar.copy(out=dst, in_=src)
+        quantize(nc, w1_codes[:], w1_scales[:], w1_bf)
+
+        cols = PIECE // PER_COL
+        for i in range(S // PIECE):
+            nc.vector.tensor_copy(
+                parent[:, i * PIECE : (i + 1) * PIECE], t_sb[:].indirect(par_sb[:, i * cols : (i + 1) * cols])
+            )
+
+        half_cols = HALF_S // PER_COL
+        for h in range(2):
+            nc.vector.tensor_copy(
+                kept_words[h][:], xw[:].bitcast(U32).indirect(offs_sb[:, h * half_cols : (h + 1) * half_cols])
+            )
+            nc.tensor.matmul_mx(
+                out=y_ps[h][:], lhsT=w1_codes[:].bitcast(FP8X4), lhsT_scale=w1_scales[:],
+                rhs=kept_words[h][:].bitcast(FP8X4), rhs_scale=kept_scales[:, h * HALF_S : (h + 1) * HALF_S],
+                start=True, stop=True,
+            )
+
+        for i in range(S // PIECE):
+            h, c0 = divmod(i * PIECE, HALF_S)
+            total = held.tile([P, PIECE], F32, name=f"total{i}")
+            result = held.tile([P, PIECE], F32, name=f"result{i}")
+            nc.vector.tensor_tensor(total[:], y_ps[h][:, c0 : c0 + PIECE], parent[:, i * PIECE : (i + 1) * PIECE], ALU.add)
+            nc.scalar.activation(out=result[:], in_=total[:], func=ACT.Relu)
+            nc.sync.dma_start(out=out[:, i * PIECE : (i + 1) * PIECE], in_=result[:])

@@ -21,12 +21,15 @@ PER_COL = 16
 HALF_S = S // 2
 HALF_V = V // 2
 PIECE = 256
+VEC_COLS = 352
+OUT_PIECES = (256, 256, 256, 128, 128)
+ROW0 = P - 16
 
 
 def weave_views(grouped, raw):
     return (
-        grouped[:].rearrange("p (c i) j -> p c j i", i=4),
-        raw[:].rearrange("p j (c i) -> p c j i", i=4),
+        grouped.rearrange("p (c i) j -> p c j i", i=4),
+        raw.rearrange("p j (c i) -> p c j i", i=4),
     )
 
 
@@ -47,18 +50,14 @@ def tile_picked_fpn_relu_p_kernel(tc, x_words, x_scales, sT, w1, w2, offs, par, 
         xs = held.tile([P, T], U8, name="xs", align_bytes=64)
         w1_raw = held.tile([P, PACK, N], F32, name="w1_raw")
         w2_raw = held.tile([P, PACK, N], F32, name="w2_raw")
-        s_raw = [held.tile([P, PACK, HALF_V], F32, name=f"s_raw{h}") for h in range(2)]
+        s_raw = held.tile([P, PACK, V], F32, name="s_raw")
 
-        nc.vector.memset(xs[:].bitcast(I32), 0)
+        nc.vector.memset(xs[0:ROW0, :].bitcast(I32), 0)
+        nc.sync.dma_start(out=xs[ROW0:P, :].bitcast(I32), in_=x_scales[0].bitcast(I32))
+        nc.sync.dma_start(offs_sb[:], offs)
         s_rows = sT.rearrange("(p j) v -> p j v", j=PACK)
         nc.sync.dma_start(out=w2_raw[:], in_=w2.rearrange("(p j) n -> p j n", j=PACK))
-        nc.sync.dma_start(out=s_raw[0][:], in_=s_rows[:, :, 0:HALF_V])
-        nc.sync.dma_start(offs_sb[:], offs)
-        nc.sync.dma_start(out=s_raw[1][:], in_=s_rows[:, :, HALF_V:V])
-        for q in range(4):
-            nc.scalar.dma_start(
-                out=xs[32 * q : 32 * q + 4, :].bitcast(I32), in_=x_scales[0, 4 * q : 4 * q + 4, :].bitcast(I32)
-            )
+        nc.sync.dma_start(out=s_raw[:], in_=s_rows)
         nc.sync.dma_start(par_sb[:], par)
         nc.sync.dma_start(out=w1_raw[:], in_=w1.rearrange("(p j) n -> p j n", j=PACK))
         nc.sync.dma_start(out=xw[:], in_=x_words[0].rearrange("p c r -> p (c r)").bitcast(I32))
@@ -74,18 +73,29 @@ def tile_picked_fpn_relu_p_kernel(tc, x_words, x_scales, sT, w1, w2, offs, par, 
         s_scales = [held.tile([P, HALF_V], U8, name=f"s_scales{h}", align_bytes=64) for h in range(2)]
         t_sb = held.tile([P, V], F32, name="t_sb", align_bytes=64)
         kept_scales = held.tile([P, S], U8, name="kept_scales", align_bytes=64)
+        kept_rows = held.tile([P, S], U8, name="kept_rows", align_bytes=64)
         kept_words = [held.tile([P, HALF_S], U32, name=f"kept_words{h}", align_bytes=64) for h in range(2)]
         parent = held.tile([P, S], F32, name="parent", align_bytes=64)
         t_ps = [psum.tile([P, HALF_V], F32, name=f"t_ps{h}") for h in range(2)]
-        y_ps = [psum.tile([P, HALF_S], F32, name=f"y_ps{h}") for h in range(2)]
+        y_ps = [psum.tile([P, PIECE], F32, name=f"y_ps{i}") for i in range(S // PIECE)]
 
-        dst, src = weave_views(w2_bf, w2_raw)
+        dst, src = weave_views(w2_bf[:], w2_raw[:])
         nc.scalar.activation(out=dst, in_=src, func=ACT.Copy)
-        nc.vector.tensor_copy(kept_scales[:], xs[:].indirect(offs_sb[:]))
+        nc.vector.memset(kept_scales[:].bitcast(I32), 0)
+        nc.vector.tensor_copy(kept_rows[:], xs[:].indirect(offs_sb[:]))
+        for q in range(4):
+            nc.sync.dma_start(
+                out=kept_scales[32 * q : 32 * q + 4, :].bitcast(I32),
+                in_=kept_rows[ROW0 + 4 * q : ROW0 + 4 * q + 4, :].bitcast(I32),
+            )
         quantize(nc, w2_codes[:], w2_scales[:], w2_bf)
+        dst, src = weave_views(s_bf[1][:, VEC_COLS - HALF_V :, :], s_raw[:, :, VEC_COLS:V])
+        nc.scalar.copy(out=dst, in_=src)
+        dst, src = weave_views(s_bf[0][:], s_raw[:, :, 0:HALF_V])
+        nc.vector.tensor_copy(out=dst, in_=src)
+        dst, src = weave_views(s_bf[1][:, 0 : VEC_COLS - HALF_V, :], s_raw[:, :, HALF_V:VEC_COLS])
+        nc.vector.tensor_copy(out=dst, in_=src)
         for h in range(2):
-            dst, src = weave_views(s_bf[h], s_raw[h])
-            nc.scalar.copy(out=dst, in_=src)
             quantize(nc, s_codes[h][:], s_scales[h][:], s_bf[h])
             nc.tensor.matmul_mx(
                 out=t_ps[h][:], lhsT=w2_codes[:].bitcast(FP8X4), lhsT_scale=w2_scales[:],
@@ -93,7 +103,7 @@ def tile_picked_fpn_relu_p_kernel(tc, x_words, x_scales, sT, w1, w2, offs, par, 
             )
         for h in range(2):
             nc.scalar.copy(out=t_sb[:, h * HALF_V : (h + 1) * HALF_V], in_=t_ps[h][:])
-        dst, src = weave_views(w1_bf, w1_raw)
+        dst, src = weave_views(w1_bf[:], w1_raw[:])
         nc.scalar.copy(out=dst, in_=src)
         quantize(nc, w1_codes[:], w1_scales[:], w1_bf)
 
@@ -108,16 +118,21 @@ def tile_picked_fpn_relu_p_kernel(tc, x_words, x_scales, sT, w1, w2, offs, par, 
             nc.vector.tensor_copy(
                 kept_words[h][:], xw[:].bitcast(U32).indirect(offs_sb[:, h * half_cols : (h + 1) * half_cols])
             )
-            nc.tensor.matmul_mx(
-                out=y_ps[h][:], lhsT=w1_codes[:].bitcast(FP8X4), lhsT_scale=w1_scales[:],
-                rhs=kept_words[h][:].bitcast(FP8X4), rhs_scale=kept_scales[:, h * HALF_S : (h + 1) * HALF_S],
-                start=True, stop=True,
-            )
+            for u in range(2):
+                i = 2 * h + u
+                nc.tensor.matmul_mx(
+                    out=y_ps[i][:], lhsT=w1_codes[:].bitcast(FP8X4), lhsT_scale=w1_scales[:],
+                    rhs=kept_words[h][:, u * PIECE : (u + 1) * PIECE].bitcast(FP8X4),
+                    rhs_scale=kept_scales[:, i * PIECE : (i + 1) * PIECE],
+                    start=True, stop=True,
+                )
 
-        for i in range(S // PIECE):
-            h, c0 = divmod(i * PIECE, HALF_S)
-            total = held.tile([P, PIECE], F32, name=f"total{i}")
-            result = held.tile([P, PIECE], F32, name=f"result{i}")
-            nc.vector.tensor_tensor(total[:], y_ps[h][:, c0 : c0 + PIECE], parent[:, i * PIECE : (i + 1) * PIECE], ALU.add)
+        c0 = 0
+        for i, width in enumerate(OUT_PIECES):
+            bank, b0 = divmod(c0, PIECE)
+            total = held.tile([P, width], F32, name=f"total{i}")
+            result = held.tile([P, width], F32, name=f"result{i}")
+            nc.vector.tensor_tensor(total[:], y_ps[bank][:, b0 : b0 + width], parent[:, c0 : c0 + width], ALU.add)
             nc.scalar.activation(out=result[:], in_=total[:], func=ACT.Relu)
-            nc.sync.dma_start(out=out[:, i * PIECE : (i + 1) * PIECE], in_=result[:])
+            nc.sync.dma_start(out=out[:, c0 : c0 + width], in_=result[:])
+            c0 = c0 + width

@@ -21,7 +21,7 @@ PER_COL = 16
 HALF_S = S // 2
 HALF_V = V // 2
 PIECE = 256
-VEC_COLS = 352
+VEC_COLS = 176
 OUT_PIECES = (256, 256, 256, 128, 128)
 ROW0 = P - 16
 
@@ -50,14 +50,15 @@ def tile_picked_fpn_relu_p_kernel(tc, x_words, x_scales, sT, w1, w2, offs, par, 
         xs = held.tile([P, T], U8, name="xs", align_bytes=64)
         w1_raw = held.tile([P, PACK, N], F32, name="w1_raw")
         w2_raw = held.tile([P, PACK, N], F32, name="w2_raw")
-        s_raw = held.tile([P, PACK, V], F32, name="s_raw")
+        s_raw = [held.tile([P, PACK, HALF_V], F32, name=f"s_raw{h}") for h in range(2)]
 
         nc.vector.memset(xs[0:ROW0, :].bitcast(I32), 0)
         nc.sync.dma_start(out=xs[ROW0:P, :].bitcast(I32), in_=x_scales[0].bitcast(I32))
         nc.sync.dma_start(offs_sb[:], offs)
         s_rows = sT.rearrange("(p j) v -> p j v", j=PACK)
         nc.sync.dma_start(out=w2_raw[:], in_=w2.rearrange("(p j) n -> p j n", j=PACK))
-        nc.sync.dma_start(out=s_raw[:], in_=s_rows)
+        nc.sync.dma_start(out=s_raw[0][:], in_=s_rows[:, :, 0:HALF_V])
+        nc.sync.dma_start(out=s_raw[1][:], in_=s_rows[:, :, HALF_V:V])
         nc.sync.dma_start(par_sb[:], par)
         nc.sync.dma_start(out=w1_raw[:], in_=w1.rearrange("(p j) n -> p j n", j=PACK))
         nc.sync.dma_start(out=xw[:], in_=x_words[0].rearrange("p c r -> p (c r)").bitcast(I32))
@@ -89,12 +90,12 @@ def tile_picked_fpn_relu_p_kernel(tc, x_words, x_scales, sT, w1, w2, offs, par, 
                 in_=kept_rows[ROW0 + 4 * q : ROW0 + 4 * q + 4, :].bitcast(I32),
             )
         quantize(nc, w2_codes[:], w2_scales[:], w2_bf)
-        dst, src = weave_views(s_bf[1][:, VEC_COLS - HALF_V :, :], s_raw[:, :, VEC_COLS:V])
+        dst, src = weave_views(s_bf[0][:], s_raw[0][:])
         nc.scalar.copy(out=dst, in_=src)
-        dst, src = weave_views(s_bf[0][:], s_raw[:, :, 0:HALF_V])
+        dst, src = weave_views(s_bf[1][:, 0:VEC_COLS, :], s_raw[1][:, :, 0:VEC_COLS])
         nc.vector.tensor_copy(out=dst, in_=src)
-        dst, src = weave_views(s_bf[1][:, 0 : VEC_COLS - HALF_V, :], s_raw[:, :, HALF_V:VEC_COLS])
-        nc.vector.tensor_copy(out=dst, in_=src)
+        dst, src = weave_views(s_bf[1][:, VEC_COLS:HALF_V, :], s_raw[1][:, :, VEC_COLS:HALF_V])
+        nc.scalar.copy(out=dst, in_=src)
         for h in range(2):
             quantize(nc, s_codes[h][:], s_scales[h][:], s_bf[h])
             nc.tensor.matmul_mx(
@@ -127,12 +128,18 @@ def tile_picked_fpn_relu_p_kernel(tc, x_words, x_scales, sT, w1, w2, offs, par, 
                     start=True, stop=True,
                 )
 
-        c0 = 0
-        for i, width in enumerate(OUT_PIECES):
-            bank, b0 = divmod(c0, PIECE)
-            total = held.tile([P, width], F32, name=f"total{i}")
-            result = held.tile([P, width], F32, name=f"result{i}")
-            nc.vector.tensor_tensor(total[:], y_ps[bank][:, b0 : b0 + width], parent[:, c0 : c0 + width], ALU.add)
+        last = S - PIECE
+        for c0 in range(0, last, PIECE):
+            total = held.tile([P, PIECE], F32, name=f"total{c0}")
+            result = held.tile([P, PIECE], F32, name=f"result{c0}")
+            nc.vector.tensor_tensor(total[:], y_ps[c0 // PIECE][:], parent[:, c0 : c0 + PIECE], ALU.add)
             nc.scalar.activation(out=result[:], in_=total[:], func=ACT.Relu)
-            nc.sync.dma_start(out=out[:, c0 : c0 + width], in_=result[:])
-            c0 = c0 + width
+            nc.sync.dma_start(out=out[:, c0 : c0 + PIECE], in_=result[:])
+        total = held.tile([P, PIECE], F32, name="total_last")
+        result = held.tile([P, PIECE], F32, name="result_last")
+        halves = (slice(0, PIECE // 2), slice(PIECE // 2, PIECE))
+        for part in halves:
+            nc.vector.tensor_tensor(total[:, part], y_ps[-1][:, part], parent[:, last:S][:, part], ALU.add)
+        for part in halves:
+            nc.vector.tensor_scalar_max(result[:, part], total[:, part], 0.0)
+        nc.sync.dma_start(out=out[:, last:S], in_=result[:])

@@ -21,8 +21,7 @@ PER_COL = 16
 HALF_S = S // 2
 HALF_V = V // 2
 PIECE = 256
-VEC_COLS = 176
-OUT_PIECES = (256, 256, 256, 128, 128)
+T_PIECES = ((0, 128), (128, 256), (256, 384), (384, 512))
 ROW0 = P - 16
 
 
@@ -34,7 +33,7 @@ def weave_views(grouped, raw):
 
 
 def quantize(nc, codes, scales, grouped):
-    nc.vector.quantize_mx(out=codes.bitcast(FP8X4), scales=scales, in_=grouped[:].rearrange("p c j -> p (c j)"))
+    nc.vector.quantize_mx(out=codes.bitcast(FP8X4), scales=scales, in_=grouped.rearrange("p c j -> p (c j)"))
 
 
 def tile_picked_fpn_relu_p_kernel(tc, x_words, x_scales, sT, w1, w2, offs, par, out):
@@ -48,36 +47,34 @@ def tile_picked_fpn_relu_p_kernel(tc, x_words, x_scales, sT, w1, w2, offs, par, 
         par_sb = lists.tile([P, S // PER_COL], U16, name="par_sb")
         xw = held.tile([P, T], I32, name="xw", align_bytes=64)
         xs = held.tile([P, T], U8, name="xs", align_bytes=64)
-        w1_raw = held.tile([P, PACK, N], F32, name="w1_raw")
+        w1_raw = held.tile([P, PACK, N], F32, name="w1_raw", tag="shared", align_bytes=64)
         w2_raw = held.tile([P, PACK, N], F32, name="w2_raw")
-        s_raw = [held.tile([P, PACK, HALF_V], F32, name=f"s_raw{h}") for h in range(2)]
+        s_raw = held.tile([P, PACK, V], F32, name="s_raw")
 
         nc.vector.memset(xs[0:ROW0, :].bitcast(I32), 0)
         nc.sync.dma_start(out=xs[ROW0:P, :].bitcast(I32), in_=x_scales[0].bitcast(I32))
         nc.sync.dma_start(offs_sb[:], offs)
         s_rows = sT.rearrange("(p j) v -> p j v", j=PACK)
         nc.sync.dma_start(out=w2_raw[:], in_=w2.rearrange("(p j) n -> p j n", j=PACK))
-        nc.sync.dma_start(out=s_raw[0][:], in_=s_rows[:, :, 0:HALF_V])
-        nc.sync.dma_start(out=s_raw[1][:], in_=s_rows[:, :, HALF_V:V])
+        nc.sync.dma_start(out=s_raw[:], in_=s_rows)
         nc.sync.dma_start(par_sb[:], par)
-        nc.sync.dma_start(out=w1_raw[:], in_=w1.rearrange("(p j) n -> p j n", j=PACK))
         nc.sync.dma_start(out=xw[:], in_=x_words[0].rearrange("p c r -> p (c r)").bitcast(I32))
+        nc.sync.dma_start(out=w1_raw[:], in_=w1.rearrange("(p j) n -> p j n", j=PACK))
 
         w1_bf = held.tile([P, N, PACK], BF16, name="w1_bf", align_bytes=64)
         w2_bf = held.tile([P, N, PACK], BF16, name="w2_bf", align_bytes=64)
-        s_bf = [held.tile([P, HALF_V, PACK], BF16, name=f"s_bf{h}", align_bytes=64) for h in range(2)]
+        s_bf = held.tile([P, V, PACK], BF16, name="s_bf", align_bytes=64)
         w1_codes = held.tile([P, N], U32, name="w1_codes", align_bytes=64)
         w1_scales = held.tile([P, N], U8, name="w1_scales", align_bytes=64)
         w2_codes = held.tile([P, N], U32, name="w2_codes", align_bytes=64)
         w2_scales = held.tile([P, N], U8, name="w2_scales", align_bytes=64)
-        s_codes = [held.tile([P, HALF_V], U32, name=f"s_codes{h}", align_bytes=64) for h in range(2)]
-        s_scales = [held.tile([P, HALF_V], U8, name=f"s_scales{h}", align_bytes=64) for h in range(2)]
+        s_codes = held.tile([P, V], U32, name="s_codes", align_bytes=64)
+        s_scales = held.tile([P, V], U8, name="s_scales", align_bytes=64)
         t_sb = held.tile([P, V], F32, name="t_sb", align_bytes=64)
         kept_scales = held.tile([P, S], U8, name="kept_scales", align_bytes=64)
         kept_rows = held.tile([P, S], U8, name="kept_rows", align_bytes=64)
-        kept_words = [held.tile([P, HALF_S], U32, name=f"kept_words{h}", align_bytes=64) for h in range(2)]
         parent = held.tile([P, S], F32, name="parent", align_bytes=64)
-        t_ps = [psum.tile([P, HALF_V], F32, name=f"t_ps{h}") for h in range(2)]
+        t_ps = [psum.tile([P, b - a], F32, name=f"t_ps{a}") for a, b in T_PIECES]
         y_ps = [psum.tile([P, PIECE], F32, name=f"y_ps{i}") for i in range(S // PIECE)]
 
         dst, src = weave_views(w2_bf[:], w2_raw[:])
@@ -89,24 +86,24 @@ def tile_picked_fpn_relu_p_kernel(tc, x_words, x_scales, sT, w1, w2, offs, par, 
                 out=kept_scales[32 * q : 32 * q + 4, :].bitcast(I32),
                 in_=kept_rows[ROW0 + 4 * q : ROW0 + 4 * q + 4, :].bitcast(I32),
             )
-        quantize(nc, w2_codes[:], w2_scales[:], w2_bf)
-        dst, src = weave_views(s_bf[0][:], s_raw[0][:])
-        nc.scalar.copy(out=dst, in_=src)
-        dst, src = weave_views(s_bf[1][:, 0:VEC_COLS, :], s_raw[1][:, :, 0:VEC_COLS])
-        nc.vector.tensor_copy(out=dst, in_=src)
-        dst, src = weave_views(s_bf[1][:, VEC_COLS:HALF_V, :], s_raw[1][:, :, VEC_COLS:HALF_V])
-        nc.scalar.copy(out=dst, in_=src)
-        for h in range(2):
-            quantize(nc, s_codes[h][:], s_scales[h][:], s_bf[h])
+        quantize(nc, w2_codes[:], w2_scales[:], w2_bf[:])
+        for i, (a, b) in enumerate(T_PIECES):
+            dst, src = weave_views(s_bf[:, a:b, :], s_raw[:, :, a:b])
+            if i < 2:
+                nc.vector.tensor_copy(out=dst, in_=src)
+            else:
+                nc.scalar.copy(out=dst, in_=src)
+        for (a, b), bank in zip(T_PIECES, t_ps):
+            quantize(nc, s_codes[:, a:b], s_scales[:, a:b], s_bf[:, a:b, :])
             nc.tensor.matmul_mx(
-                out=t_ps[h][:], lhsT=w2_codes[:].bitcast(FP8X4), lhsT_scale=w2_scales[:],
-                rhs=s_codes[h][:].bitcast(FP8X4), rhs_scale=s_scales[h][:], start=True, stop=True,
+                out=bank[:], lhsT=w2_codes[:].bitcast(FP8X4), lhsT_scale=w2_scales[:],
+                rhs=s_codes[:, a:b].bitcast(FP8X4), rhs_scale=s_scales[:, a:b], start=True, stop=True,
             )
-        for h in range(2):
-            nc.scalar.copy(out=t_sb[:, h * HALF_V : (h + 1) * HALF_V], in_=t_ps[h][:])
+        for (a, b), bank in zip(T_PIECES, t_ps):
+            nc.scalar.copy(out=t_sb[:, a:b], in_=bank[:])
         dst, src = weave_views(w1_bf[:], w1_raw[:])
         nc.scalar.copy(out=dst, in_=src)
-        quantize(nc, w1_codes[:], w1_scales[:], w1_bf)
+        quantize(nc, w1_codes[:], w1_scales[:], w1_bf[:])
 
         cols = PIECE // PER_COL
         for i in range(S // PIECE):
@@ -115,6 +112,10 @@ def tile_picked_fpn_relu_p_kernel(tc, x_words, x_scales, sT, w1, w2, offs, par, 
             )
 
         half_cols = HALF_S // PER_COL
+        kept_words = [
+            held.tile([P, HALF_S], U32, name="kept_words0", align_bytes=64),
+            held.tile([P, HALF_S], U32, name="kept_words1", tag="shared", align_bytes=64),
+        ]
         for h in range(2):
             nc.vector.tensor_copy(
                 kept_words[h][:], xw[:].bitcast(U32).indirect(offs_sb[:, h * half_cols : (h + 1) * half_cols])

@@ -68,10 +68,9 @@ def tile_picked_fpn_relu_p_kernel(tc, x_words, x_scales, sT, w1, w2, offs, par, 
         w1_scales = held.tile([P, N], U8, name="w1_scales", align_bytes=64)
         w2_codes = held.tile([P, N], U32, name="w2_codes", align_bytes=64)
         w2_scales = held.tile([P, N], U8, name="w2_scales", align_bytes=64)
-        s_codes = held.tile([P, V], U32, name="s_codes", align_bytes=64)
+        s_codes = held.tile([P, V], U32, name="s_codes", tag="coarse", align_bytes=64)
         s_scales = held.tile([P, V], U8, name="s_scales", align_bytes=64)
         t_sb = held.tile([P, V], F32, name="t_sb", align_bytes=64)
-        kept_scales = held.tile([P, S], U8, name="kept_scales", align_bytes=64)
         kept_rows = held.tile([P, S], U8, name="kept_rows", align_bytes=64)
         parent = held.tile([P, S], F32, name="parent", align_bytes=64)
         t_ps = [psum.tile([P, b - a], F32, name=f"t_ps{a}") for a, b in T_PIECES]
@@ -79,13 +78,7 @@ def tile_picked_fpn_relu_p_kernel(tc, x_words, x_scales, sT, w1, w2, offs, par, 
 
         dst, src = weave_views(w2_bf[:], w2_raw[:])
         nc.scalar.activation(out=dst, in_=src, func=ACT.Copy)
-        nc.vector.memset(kept_scales[:].bitcast(I32), 0)
         nc.vector.tensor_copy(kept_rows[:], xs[:].indirect(offs_sb[:]))
-        for q in range(4):
-            nc.sync.dma_start(
-                out=kept_scales[32 * q : 32 * q + 4, :].bitcast(I32),
-                in_=kept_rows[ROW0 + 4 * q : ROW0 + 4 * q + 4, :].bitcast(I32),
-            )
         quantize(nc, w2_codes[:], w2_scales[:], w2_bf[:])
         for i, (a, b) in enumerate(T_PIECES):
             dst, src = weave_views(s_bf[:, a:b, :], s_raw[:, :, a:b])
@@ -101,6 +94,13 @@ def tile_picked_fpn_relu_p_kernel(tc, x_words, x_scales, sT, w1, w2, offs, par, 
             )
         for (a, b), bank in zip(T_PIECES, t_ps):
             nc.scalar.copy(out=t_sb[:, a:b], in_=bank[:])
+        kept_scales = held.tile([P, S], U8, name="kept_scales", tag="coarse", align_bytes=64)
+        nc.vector.memset(kept_scales[:].bitcast(I32), 0)
+        for q in range(4):
+            nc.scalar.dma_start(
+                out=kept_scales[32 * q : 32 * q + 4, :].bitcast(I32),
+                in_=kept_rows[ROW0 + 4 * q : ROW0 + 4 * q + 4, :].bitcast(I32),
+            )
         dst, src = weave_views(w1_bf[:], w1_raw[:])
         nc.scalar.copy(out=dst, in_=src)
         quantize(nc, w1_codes[:], w1_scales[:], w1_bf[:])

@@ -22,7 +22,10 @@ HALF_S = S // 2
 HALF_V = V // 2
 PIECE = 256
 T_PIECES = ((0, 128), (128, 256), (256, 384), (384, 512))
+WEAVES = ((0, 128, True), (256, 384, False), (128, 256, True), (384, 448, False), (448, 512, True))
 ROW0 = P - 16
+Y_PASSES = (((0, 256, "ya0"), (256, 512, "ya1")), ((512, 640, "yb0"), (640, 768, "yb1"), (768, 896, "t128"), (896, 1024, "t0")))
+OUT_PIECES = ((0, 256, False), (256, 512, False), (512, 768, True), (768, 1024, True))
 
 
 def weave_views(grouped, raw):
@@ -47,7 +50,7 @@ def tile_picked_fpn_relu_p_kernel(tc, x_words, x_scales, sT, w1, w2, offs, par, 
         par_sb = lists.tile([P, S // PER_COL], U16, name="par_sb")
         xw = held.tile([P, T], I32, name="xw", align_bytes=64)
         xs = held.tile([P, T], U8, name="xs", align_bytes=64)
-        w1_raw = held.tile([P, PACK, N], F32, name="w1_raw", tag="shared", align_bytes=64)
+        w1_raw = held.tile([P, PACK, N], F32, name="w1_raw", align_bytes=64)
         w2_raw = held.tile([P, PACK, N], F32, name="w2_raw")
         s_raw = held.tile([P, PACK, V], F32, name="s_raw")
 
@@ -57,9 +60,9 @@ def tile_picked_fpn_relu_p_kernel(tc, x_words, x_scales, sT, w1, w2, offs, par, 
         s_rows = sT.rearrange("(p j) v -> p j v", j=PACK)
         nc.sync.dma_start(out=w2_raw[:], in_=w2.rearrange("(p j) n -> p j n", j=PACK))
         nc.sync.dma_start(out=s_raw[:], in_=s_rows)
+        nc.sync.dma_start(out=w1_raw[:], in_=w1.rearrange("(p j) n -> p j n", j=PACK))
         nc.sync.dma_start(par_sb[:], par)
         nc.sync.dma_start(out=xw[:], in_=x_words[0].rearrange("p c r -> p (c r)").bitcast(I32))
-        nc.sync.dma_start(out=w1_raw[:], in_=w1.rearrange("(p j) n -> p j n", j=PACK))
 
         w1_bf = held.tile([P, N, PACK], BF16, name="w1_bf", align_bytes=64)
         w2_bf = held.tile([P, N, PACK], BF16, name="w2_bf", align_bytes=64)
@@ -73,16 +76,15 @@ def tile_picked_fpn_relu_p_kernel(tc, x_words, x_scales, sT, w1, w2, offs, par, 
         t_sb = held.tile([P, V], F32, name="t_sb", align_bytes=64)
         kept_rows = held.tile([P, S], U8, name="kept_rows", align_bytes=64)
         parent = held.tile([P, S], F32, name="parent", align_bytes=64)
-        t_ps = [psum.tile([P, b - a], F32, name=f"t_ps{a}") for a, b in T_PIECES]
-        y_ps = [psum.tile([P, PIECE], F32, name=f"y_ps{i}") for i in range(S // PIECE)]
+        t_ps = [psum.tile([P, b - a], F32, name=f"t_ps{a}", tag=f"t{a}") for a, b in T_PIECES]
 
         dst, src = weave_views(w2_bf[:], w2_raw[:])
         nc.scalar.activation(out=dst, in_=src, func=ACT.Copy)
         nc.vector.tensor_copy(kept_rows[:], xs[:].indirect(offs_sb[:]))
         quantize(nc, w2_codes[:], w2_scales[:], w2_bf[:])
-        for i, (a, b) in enumerate(T_PIECES):
+        for a, b, on_vector in WEAVES:
             dst, src = weave_views(s_bf[:, a:b, :], s_raw[:, :, a:b])
-            if i < 2:
+            if on_vector:
                 nc.vector.tensor_copy(out=dst, in_=src)
             else:
                 nc.scalar.copy(out=dst, in_=src)
@@ -92,55 +94,51 @@ def tile_picked_fpn_relu_p_kernel(tc, x_words, x_scales, sT, w1, w2, offs, par, 
                 out=bank[:], lhsT=w2_codes[:].bitcast(FP8X4), lhsT_scale=w2_scales[:],
                 rhs=s_codes[:, a:b].bitcast(FP8X4), rhs_scale=s_scales[:, a:b], start=True, stop=True,
             )
-        for (a, b), bank in zip(T_PIECES, t_ps):
+        for (a, b), bank in zip(T_PIECES[:3], t_ps):
             nc.scalar.copy(out=t_sb[:, a:b], in_=bank[:])
         kept_scales = held.tile([P, S], U8, name="kept_scales", tag="coarse", align_bytes=64)
-        nc.vector.memset(kept_scales[:].bitcast(I32), 0)
+        nc.gpsimd.memset(kept_scales[:].bitcast(I32), 0)
         for q in range(4):
             nc.scalar.dma_start(
                 out=kept_scales[32 * q : 32 * q + 4, :].bitcast(I32),
                 in_=kept_rows[ROW0 + 4 * q : ROW0 + 4 * q + 4, :].bitcast(I32),
             )
         dst, src = weave_views(w1_bf[:], w1_raw[:])
-        nc.scalar.copy(out=dst, in_=src)
+        nc.vector.tensor_copy(out=dst, in_=src)
+        nc.vector.tensor_copy(out=t_sb[:, 384:512], in_=t_ps[3][:])
         quantize(nc, w1_codes[:], w1_scales[:], w1_bf[:])
 
-        cols = PIECE // PER_COL
-        for i in range(S // PIECE):
-            nc.vector.tensor_copy(
-                parent[:, i * PIECE : (i + 1) * PIECE], t_sb[:].indirect(par_sb[:, i * cols : (i + 1) * cols])
-            )
+        for a, b in ((0, 352), (352, 704), (704, 1024)):
+            nc.vector.tensor_copy(parent[:, a:b], t_sb[:].indirect(par_sb[:, a // PER_COL : b // PER_COL]))
 
         half_cols = HALF_S // PER_COL
-        kept_words = [
-            held.tile([P, HALF_S], U32, name="kept_words0", align_bytes=64),
-            held.tile([P, HALF_S], U32, name="kept_words1", tag="shared", align_bytes=64),
-        ]
+        kept_words = [held.tile([P, HALF_S], U32, name=f"kept_words{h}", align_bytes=64) for h in range(2)]
+        y_at = []
         for h in range(2):
             nc.vector.tensor_copy(
                 kept_words[h][:], xw[:].bitcast(U32).indirect(offs_sb[:, h * half_cols : (h + 1) * half_cols])
             )
-            for u in range(2):
-                i = 2 * h + u
+            for a, b, tag in Y_PASSES[h]:
+                bank = psum.tile([P, b - a], F32, name=f"y_ps{a}", tag=tag)
                 nc.tensor.matmul_mx(
-                    out=y_ps[i][:], lhsT=w1_codes[:].bitcast(FP8X4), lhsT_scale=w1_scales[:],
-                    rhs=kept_words[h][:, u * PIECE : (u + 1) * PIECE].bitcast(FP8X4),
-                    rhs_scale=kept_scales[:, i * PIECE : (i + 1) * PIECE],
-                    start=True, stop=True,
+                    out=bank[:], lhsT=w1_codes[:].bitcast(FP8X4), lhsT_scale=w1_scales[:],
+                    rhs=kept_words[h][:, a - h * HALF_S : b - h * HALF_S].bitcast(FP8X4),
+                    rhs_scale=kept_scales[:, a:b], start=True, stop=True,
                 )
+                y_at.append((bank, a, b))
 
-        last = S - PIECE
-        for c0 in range(0, last, PIECE):
-            total = held.tile([P, PIECE], F32, name=f"total{c0}")
-            result = held.tile([P, PIECE], F32, name=f"result{c0}")
-            nc.vector.tensor_tensor(total[:], y_ps[c0 // PIECE][:], parent[:, c0 : c0 + PIECE], ALU.add)
-            nc.scalar.activation(out=result[:], in_=total[:], func=ACT.Relu)
-            nc.sync.dma_start(out=out[:, c0 : c0 + PIECE], in_=result[:])
-        total = held.tile([P, PIECE], F32, name="total_last")
-        result = held.tile([P, PIECE], F32, name="result_last")
-        halves = (slice(0, PIECE // 2), slice(PIECE // 2, PIECE))
-        for part in halves:
-            nc.vector.tensor_tensor(total[:, part], y_ps[-1][:, part], parent[:, last:S][:, part], ALU.add)
-        for part in halves:
-            nc.vector.tensor_scalar_max(result[:, part], total[:, part], 0.0)
-        nc.sync.dma_start(out=out[:, last:S], in_=result[:])
+        late = []
+        for a, b, on_vector in OUT_PIECES:
+            total = held.tile([P, b - a], F32, name=f"total{a}")
+            result = held.tile([P, b - a], F32, name=f"result{a}")
+            for bank, c, d in y_at:
+                if a <= c < b:
+                    nc.vector.tensor_tensor(total[:, c - a : d - a], bank[:], parent[:, c:d], ALU.add)
+            if on_vector:
+                late.append((a, b, total, result))
+            else:
+                nc.scalar.activation(out=result[:], in_=total[:], func=ACT.Relu)
+                nc.sync.dma_start(out=out[:, a:b], in_=result[:])
+        for a, b, total, result in late:
+            nc.vector.tensor_scalar_max(result[:], total[:], 0.0)
+            nc.sync.dma_start(out=out[:, a:b], in_=result[:])

@@ -71,7 +71,7 @@ def tile_picked_fpn_relu_p_kernel(tc, x_words, x_scales, sT, w1, w2, offs, par, 
         w1_scales = held.tile([P, N], U8, name="w1_scales", align_bytes=64)
         w2_codes = held.tile([P, N], U32, name="w2_codes", align_bytes=64)
         w2_scales = held.tile([P, N], U8, name="w2_scales", align_bytes=64)
-        s_codes = held.tile([P, V], U32, name="s_codes", tag="coarse", align_bytes=64)
+        s_codes = held.tile([P, V], U32, name="s_codes", align_bytes=64)
         s_scales = held.tile([P, V], U8, name="s_scales", align_bytes=64)
         t_sb = held.tile([P, V], F32, name="t_sb", align_bytes=64)
         kept_rows = held.tile([P, S], U8, name="kept_rows", align_bytes=64)
@@ -96,10 +96,10 @@ def tile_picked_fpn_relu_p_kernel(tc, x_words, x_scales, sT, w1, w2, offs, par, 
             )
         for (a, b), bank in zip(T_PIECES[:3], t_ps):
             nc.scalar.copy(out=t_sb[:, a:b], in_=bank[:])
-        kept_scales = held.tile([P, S], U8, name="kept_scales", tag="coarse", align_bytes=64)
-        nc.gpsimd.memset(kept_scales[:].bitcast(I32), 0)
+        kept_scales = held.tile([P, S], U8, name="kept_scales", align_bytes=64)
+        nc.vector.memset(kept_scales[:].bitcast(I32), 0)
         for q in range(4):
-            nc.scalar.dma_start(
+            nc.sync.dma_start(
                 out=kept_scales[32 * q : 32 * q + 4, :].bitcast(I32),
                 in_=kept_rows[ROW0 + 4 * q : ROW0 + 4 * q + 4, :].bitcast(I32),
             )

@@ -24,7 +24,10 @@ PIECE = 256
 T_PIECES = ((0, 128), (128, 256), (256, 384), (384, 512))
 WEAVES = ((0, 128, True), (256, 384, False), (128, 256, True), (384, 448, False), (448, 512, True))
 ROW0 = P - 16
-Y_PASSES = (((0, 256, "ya0"), (256, 512, "ya1")), ((512, 640, "yb0"), (640, 768, "yb1"), (768, 896, "t128"), (896, 1024, "t0")))
+Y_PASSES = (
+    ((0, 128, "ya2"), (256, 512, "ya0"), (128, 256, "ya1")),
+    ((512, 640, "t0"), (640, 768, "t128"), (768, 896, "t256"), (896, 1024, "t384")),
+)
 OUT_PIECES = ((0, 256, False), (256, 512, False), (512, 768, True), (768, 1024, True))
 
 
@@ -50,7 +53,7 @@ def tile_picked_fpn_relu_p_kernel(tc, x_words, x_scales, sT, w1, w2, offs, par, 
         par_sb = lists.tile([P, S // PER_COL], U16, name="par_sb")
         xw = held.tile([P, T], I32, name="xw", align_bytes=64)
         xs = held.tile([P, T], U8, name="xs", align_bytes=64)
-        w1_raw = held.tile([P, PACK, N], F32, name="w1_raw", align_bytes=64)
+        w1_raw = held.tile([P, PACK, N], F32, name="w1_raw", tag="shared", align_bytes=64)
         w2_raw = held.tile([P, PACK, N], F32, name="w2_raw")
         s_raw = held.tile([P, PACK, V], F32, name="s_raw")
 
@@ -60,9 +63,9 @@ def tile_picked_fpn_relu_p_kernel(tc, x_words, x_scales, sT, w1, w2, offs, par, 
         s_rows = sT.rearrange("(p j) v -> p j v", j=PACK)
         nc.sync.dma_start(out=w2_raw[:], in_=w2.rearrange("(p j) n -> p j n", j=PACK))
         nc.sync.dma_start(out=s_raw[:], in_=s_rows)
-        nc.sync.dma_start(out=w1_raw[:], in_=w1.rearrange("(p j) n -> p j n", j=PACK))
         nc.sync.dma_start(par_sb[:], par)
         nc.sync.dma_start(out=xw[:], in_=x_words[0].rearrange("p c r -> p (c r)").bitcast(I32))
+        nc.sync.dma_start(out=w1_raw[:], in_=w1.rearrange("(p j) n -> p j n", j=PACK))
 
         w1_bf = held.tile([P, N, PACK], BF16, name="w1_bf", align_bytes=64)
         w2_bf = held.tile([P, N, PACK], BF16, name="w2_bf", align_bytes=64)
@@ -103,16 +106,19 @@ def tile_picked_fpn_relu_p_kernel(tc, x_words, x_scales, sT, w1, w2, offs, par, 
                 out=kept_scales[32 * q : 32 * q + 4, :].bitcast(I32),
                 in_=kept_rows[ROW0 + 4 * q : ROW0 + 4 * q + 4, :].bitcast(I32),
             )
-        dst, src = weave_views(w1_bf[:], w1_raw[:])
-        nc.vector.tensor_copy(out=dst, in_=src)
         nc.vector.tensor_copy(out=t_sb[:, 384:512], in_=t_ps[3][:])
+        dst, src = weave_views(w1_bf[:], w1_raw[:])
+        nc.scalar.copy(out=dst, in_=src)
         quantize(nc, w1_codes[:], w1_scales[:], w1_bf[:])
 
-        for a, b in ((0, 352), (352, 704), (704, 1024)):
+        for a, b in ((128, 576), (576, 1024)):
             nc.vector.tensor_copy(parent[:, a:b], t_sb[:].indirect(par_sb[:, a // PER_COL : b // PER_COL]))
 
         half_cols = HALF_S // PER_COL
-        kept_words = [held.tile([P, HALF_S], U32, name=f"kept_words{h}", align_bytes=64) for h in range(2)]
+        kept_words = [
+            held.tile([P, HALF_S], U32, name="kept_words0", align_bytes=64),
+            held.tile([P, HALF_S], U32, name="kept_words1", tag="shared", align_bytes=64),
+        ]
         y_at = []
         for h in range(2):
             nc.vector.tensor_copy(
@@ -127,18 +133,34 @@ def tile_picked_fpn_relu_p_kernel(tc, x_words, x_scales, sT, w1, w2, offs, par, 
                 )
                 y_at.append((bank, a, b))
 
-        late = []
-        for a, b, on_vector in OUT_PIECES:
-            total = held.tile([P, b - a], F32, name=f"total{a}")
-            result = held.tile([P, b - a], F32, name=f"result{a}")
-            for bank, c, d in y_at:
-                if a <= c < b:
-                    nc.vector.tensor_tensor(total[:, c - a : d - a], bank[:], parent[:, c:d], ALU.add)
+        total = held.tile([P, S], F32, name="total")
+        result = held.tile([P, S], F32, name="result")
+
+        def add(n):
+            bank, c, d = y_at[n]
+            nc.vector.tensor_tensor(total[:, c:d], bank[:], parent[:, c:d], ALU.add)
+
+        def gather_add(n):
+            bank, c, d = y_at[n]
+            y_sb = held.tile([P, d - c], F32, name=f"y_sb{n}")
+            nc.scalar.copy(out=y_sb[:], in_=bank[:])
+            nc.vector.tensor_tensor(total[:, c:d], t_sb[:].indirect(par_sb[:, c // PER_COL : d // PER_COL]), y_sb[:], ALU.add)
+
+        def finish(a, b, on_vector):
             if on_vector:
-                late.append((a, b, total, result))
+                nc.vector.tensor_scalar_max(result[:, a:b], total[:, a:b], 0.0)
             else:
-                nc.scalar.activation(out=result[:], in_=total[:], func=ACT.Relu)
-                nc.sync.dma_start(out=out[:, a:b], in_=result[:])
-        for a, b, total, result in late:
-            nc.vector.tensor_scalar_max(result[:], total[:], 0.0)
-            nc.sync.dma_start(out=out[:, a:b], in_=result[:])
+                nc.scalar.activation(out=result[:, a:b], in_=total[:, a:b], func=ACT.Relu)
+            nc.sync.dma_start(out=out[:, a:b], in_=result[:, a:b])
+
+        add(1)
+        finish(256, 512, False)
+        add(2)
+        gather_add(0)
+        finish(0, 256, False)
+        add(3)
+        add(4)
+        add(5)
+        add(6)
+        finish(512, 768, True)
+        finish(768, 1024, True)

@@ -58,7 +58,7 @@ def tile_picked_fpn_relu_p_kernel(tc, x_words, x_scales, sT, w1, w2, offs, par, 
         s_raw = held.tile([P, PACK, V], F32, name="s_raw")
 
         nc.vector.memset(xs[0:ROW0, :].bitcast(I32), 0)
-        nc.sync.dma_start(out=xs[ROW0:P, :].bitcast(I32), in_=x_scales[0].bitcast(I32))
+        nc.scalar.dma_start(out=xs[ROW0:P, :].bitcast(I32), in_=x_scales[0].bitcast(I32))
         nc.sync.dma_start(offs_sb[:], offs)
         s_rows = sT.rearrange("(p j) v -> p j v", j=PACK)
         nc.sync.dma_start(out=w2_raw[:], in_=w2.rearrange("(p j) n -> p j n", j=PACK))

@@ -146,21 +146,30 @@ def tile_picked_fpn_relu_p_kernel(tc, x_words, x_scales, sT, w1, w2, offs, par, 
             nc.scalar.copy(out=y_sb[:], in_=bank[:])
             nc.vector.tensor_tensor(total[:, c:d], t_sb[:].indirect(par_sb[:, c // PER_COL : d // PER_COL]), y_sb[:], ALU.add)
 
-        def finish(a, b, on_vector):
+        def relu(a, b, on_vector):
             if on_vector:
                 nc.vector.tensor_scalar_max(result[:, a:b], total[:, a:b], 0.0)
             else:
                 nc.scalar.activation(out=result[:, a:b], in_=total[:, a:b], func=ACT.Relu)
+
+        def store(a, b):
             nc.sync.dma_start(out=out[:, a:b], in_=result[:, a:b])
 
         add(1)
-        finish(256, 512, False)
+        relu(256, 512, False)
+        store(256, 512)
         add(2)
+        relu(128, 256, False)
         gather_add(0)
-        finish(0, 256, False)
+        relu(0, 128, False)
+        store(0, 256)
         add(3)
+        relu(512, 640, False)
         add(4)
+        relu(640, 768, False)
+        store(512, 768)
         add(5)
         add(6)
-        finish(512, 768, True)
-        finish(768, 1024, True)
+        relu(768, 896, True)
+        relu(896, 1024, True)
+        store(768, 1024)

@@ -23,12 +23,8 @@ HALF_V = V // 2
 PIECE = 256
 T_PIECES = ((0, 128), (128, 256), (256, 384), (384, 512))
 WEAVES = ((0, 128, True), (256, 384, False), (128, 256, True), (384, 448, False), (448, 512, True))
-ROW0 = P - 16
-Y_PASSES = (
-    ((0, 128, "ya2"), (256, 512, "ya0"), (128, 256, "ya1")),
-    ((512, 640, "t0"), (640, 768, "t128"), (768, 896, "t256"), (896, 1024, "t384")),
-)
-OUT_PIECES = ((0, 256, False), (256, 512, False), (512, 768, True), (768, 1024, True))
+ROW0 = 32
+Y_PASSES = (((0, 256, "y0"),), ((256, 512, "y1"),), ((512, 768, "y2"),), ((768, 896, "t0"), (896, 1024, "t128")))
 
 
 def weave_views(grouped, raw):
@@ -52,24 +48,24 @@ def tile_picked_fpn_relu_p_kernel(tc, x_words, x_scales, sT, w1, w2, offs, par, 
         offs_sb = lists.tile([P, S // PER_COL], U16, name="offs_sb")
         par_sb = lists.tile([P, S // PER_COL], U16, name="par_sb")
         xw = held.tile([P, T], I32, name="xw", align_bytes=64)
-        xs = held.tile([P, T], U8, name="xs", align_bytes=64)
+        xs = held.tile([P, T], U8, name="xs", tag="rows", align_bytes=64)
         w1_raw = held.tile([P, PACK, N], F32, name="w1_raw", tag="shared", align_bytes=64)
         w2_raw = held.tile([P, PACK, N], F32, name="w2_raw")
         s_raw = held.tile([P, PACK, V], F32, name="s_raw")
 
-        nc.vector.memset(xs[0:ROW0, :].bitcast(I32), 0)
-        nc.scalar.dma_start(out=xs[ROW0:P, :].bitcast(I32), in_=x_scales[0].bitcast(I32))
-        nc.sync.dma_start(offs_sb[:], offs)
+        nc.vector.memset(xs[:].bitcast(I32), 0)
         s_rows = sT.rearrange("(p j) v -> p j v", j=PACK)
         nc.sync.dma_start(out=w2_raw[:], in_=w2.rearrange("(p j) n -> p j n", j=PACK))
         nc.sync.dma_start(out=s_raw[:], in_=s_rows)
+        nc.sync.dma_start(offs_sb[:], offs)
         nc.sync.dma_start(par_sb[:], par)
+        nc.sync.dma_start(out=xs[ROW0 : ROW0 + 64 : 4, :].bitcast(I32), in_=x_scales[0].bitcast(I32))
         nc.sync.dma_start(out=xw[:], in_=x_words[0].rearrange("p c r -> p (c r)").bitcast(I32))
         nc.sync.dma_start(out=w1_raw[:], in_=w1.rearrange("(p j) n -> p j n", j=PACK))
 
         w1_bf = held.tile([P, N, PACK], BF16, name="w1_bf", align_bytes=64)
         w2_bf = held.tile([P, N, PACK], BF16, name="w2_bf", align_bytes=64)
-        s_bf = held.tile([P, V, PACK], BF16, name="s_bf", align_bytes=64)
+        s_bf = held.tile([P, V, PACK], BF16, name="s_bf", tag="woven", align_bytes=64)
         w1_codes = held.tile([P, N], U32, name="w1_codes", align_bytes=64)
         w1_scales = held.tile([P, N], U8, name="w1_scales", align_bytes=64)
         w2_codes = held.tile([P, N], U32, name="w2_codes", align_bytes=64)
@@ -77,13 +73,11 @@ def tile_picked_fpn_relu_p_kernel(tc, x_words, x_scales, sT, w1, w2, offs, par, 
         s_codes = held.tile([P, V], U32, name="s_codes", align_bytes=64)
         s_scales = held.tile([P, V], U8, name="s_scales", align_bytes=64)
         t_sb = held.tile([P, V], F32, name="t_sb", align_bytes=64)
-        kept_rows = held.tile([P, S], U8, name="kept_rows", align_bytes=64)
         parent = held.tile([P, S], F32, name="parent", align_bytes=64)
         t_ps = [psum.tile([P, b - a], F32, name=f"t_ps{a}", tag=f"t{a}") for a, b in T_PIECES]
 
         dst, src = weave_views(w2_bf[:], w2_raw[:])
         nc.scalar.activation(out=dst, in_=src, func=ACT.Copy)
-        nc.vector.tensor_copy(kept_rows[:], xs[:].indirect(offs_sb[:]))
         quantize(nc, w2_codes[:], w2_scales[:], w2_bf[:])
         for a, b, on_vector in WEAVES:
             dst, src = weave_views(s_bf[:, a:b, :], s_raw[:, :, a:b])
@@ -97,79 +91,49 @@ def tile_picked_fpn_relu_p_kernel(tc, x_words, x_scales, sT, w1, w2, offs, par, 
                 out=bank[:], lhsT=w2_codes[:].bitcast(FP8X4), lhsT_scale=w2_scales[:],
                 rhs=s_codes[:, a:b].bitcast(FP8X4), rhs_scale=s_scales[:, a:b], start=True, stop=True,
             )
-        for (a, b), bank in zip(T_PIECES[:3], t_ps):
+        kept_rows = held.tile([P, S], U8, name="kept_rows", tag="woven", align_bytes=64)
+        nc.vector.tensor_copy(kept_rows[:], xs[:].indirect(offs_sb[:]))
+        for (a, b), bank in zip(T_PIECES, t_ps):
             nc.scalar.copy(out=t_sb[:, a:b], in_=bank[:])
         kept_scales = held.tile([P, S], U8, name="kept_scales", align_bytes=64)
         nc.vector.memset(kept_scales[:].bitcast(I32), 0)
         for q in range(4):
             nc.sync.dma_start(
                 out=kept_scales[32 * q : 32 * q + 4, :].bitcast(I32),
-                in_=kept_rows[ROW0 + 4 * q : ROW0 + 4 * q + 4, :].bitcast(I32),
+                in_=kept_rows[ROW0 + 16 * q : ROW0 + 16 * q + 16 : 4, :].bitcast(I32),
             )
-        nc.vector.tensor_copy(out=t_sb[:, 384:512], in_=t_ps[3][:])
         dst, src = weave_views(w1_bf[:], w1_raw[:])
         nc.scalar.copy(out=dst, in_=src)
         quantize(nc, w1_codes[:], w1_scales[:], w1_bf[:])
 
-        for a, b in ((128, 576), (576, 1024)):
-            nc.vector.tensor_copy(parent[:, a:b], t_sb[:].indirect(par_sb[:, a // PER_COL : b // PER_COL]))
+        parent_last = held.tile([P, 128], F32, name="parent_last", tag="rows", align_bytes=64)
+        nc.vector.tensor_copy(parent_last[:], t_sb[:].indirect(par_sb[:, 56:64]))
+        for a, b in ((0, 448), (448, 896)):
+            nc.scalar.activation(out=parent[:, a:b], in_=t_sb[:].indirect(par_sb[:, a // PER_COL : b // PER_COL]), func=ACT.Copy)
 
-        half_cols = HALF_S // PER_COL
-        kept_words = [
-            held.tile([P, HALF_S], U32, name="kept_words0", align_bytes=64),
-            held.tile([P, HALF_S], U32, name="kept_words1", tag="shared", align_bytes=64),
-        ]
+        total = held.tile([P, S], F32, name="total")
+        result = held.tile([P, S], F32, name="result")
         y_at = []
-        for h in range(2):
-            nc.vector.tensor_copy(
-                kept_words[h][:], xw[:].bitcast(U32).indirect(offs_sb[:, h * half_cols : (h + 1) * half_cols])
-            )
-            for a, b, tag in Y_PASSES[h]:
+        kept_late = held.tile([P, HALF_S], U32, name="kept_late", tag="shared", align_bytes=64)
+        kept_early = held.tile([P, HALF_S], U32, name="kept_early", align_bytes=64)
+        for g in range(4):
+            a0 = g * PIECE
+            kept = (kept_early, kept_late)[g // 2][:, a0 % HALF_S : a0 % HALF_S + PIECE]
+            nc.vector.tensor_copy(kept, xw[:].bitcast(U32).indirect(offs_sb[:, a0 // PER_COL : (a0 + PIECE) // PER_COL]))
+            for a, b, tag in Y_PASSES[g]:
                 bank = psum.tile([P, b - a], F32, name=f"y_ps{a}", tag=tag)
                 nc.tensor.matmul_mx(
                     out=bank[:], lhsT=w1_codes[:].bitcast(FP8X4), lhsT_scale=w1_scales[:],
-                    rhs=kept_words[h][:, a - h * HALF_S : b - h * HALF_S].bitcast(FP8X4),
+                    rhs=kept[:, a - a0 : b - a0].bitcast(FP8X4),
                     rhs_scale=kept_scales[:, a:b], start=True, stop=True,
                 )
                 y_at.append((bank, a, b))
 
-        total = held.tile([P, S], F32, name="total")
-        result = held.tile([P, S], F32, name="result")
-
-        def add(n):
-            bank, c, d = y_at[n]
-            nc.vector.tensor_tensor(total[:, c:d], bank[:], parent[:, c:d], ALU.add)
-
-        def gather_add(n):
-            bank, c, d = y_at[n]
-            y_sb = held.tile([P, d - c], F32, name=f"y_sb{n}")
-            nc.scalar.copy(out=y_sb[:], in_=bank[:])
-            nc.vector.tensor_tensor(total[:, c:d], t_sb[:].indirect(par_sb[:, c // PER_COL : d // PER_COL]), y_sb[:], ALU.add)
-
-        def relu(a, b, on_vector):
-            if on_vector:
-                nc.vector.tensor_scalar_max(result[:, a:b], total[:, a:b], 0.0)
+        for bank, c, d in y_at:
+            nc.vector.tensor_tensor(total[:, c:d], bank[:], parent[:, c:d] if d <= 896 else parent_last[:], ALU.add)
+            if d == S:
+                nc.vector.tensor_scalar_max(result[:, c:d], total[:, c:d], 0.0)
             else:
-                nc.scalar.activation(out=result[:, a:b], in_=total[:, a:b], func=ACT.Relu)
-
-        def store(a, b):
-            nc.sync.dma_start(out=out[:, a:b], in_=result[:, a:b])
-
-        add(1)
-        relu(256, 512, False)
-        store(256, 512)
-        add(2)
-        relu(128, 256, False)
-        gather_add(0)
-        relu(0, 128, False)
-        store(0, 256)
-        add(3)
-        relu(512, 640, False)
-        add(4)
-        relu(640, 768, False)
-        store(512, 768)
-        add(5)
-        add(6)
-        relu(768, 896, True)
-        relu(896, 1024, True)
-        store(768, 1024)
+                nc.scalar.activation(out=result[:, c:d], in_=total[:, c:d], func=ACT.Relu)
+            if d % PIECE == 0:
+                nc.sync.dma_start(out=out[:, d - PIECE : d], in_=result[:, d - PIECE : d])

@@ -48,7 +48,7 @@ def tile_picked_fpn_relu_p_kernel(tc, x_words, x_scales, sT, w1, w2, offs, par, 
         offs_sb = lists.tile([P, S // PER_COL], U16, name="offs_sb")
         par_sb = lists.tile([P, S // PER_COL], U16, name="par_sb")
         xw = held.tile([P, T], I32, name="xw", align_bytes=64)
-        xs = held.tile([P, T], U8, name="xs", tag="rows", align_bytes=64)
+        xs = held.tile([P, T], U8, name="xs", align_bytes=64)
         w1_raw = held.tile([P, PACK, N], F32, name="w1_raw", tag="shared", align_bytes=64)
         w2_raw = held.tile([P, PACK, N], F32, name="w2_raw")
         s_raw = held.tile([P, PACK, V], F32, name="s_raw")
@@ -106,9 +106,7 @@ def tile_picked_fpn_relu_p_kernel(tc, x_words, x_scales, sT, w1, w2, offs, par, 
         nc.scalar.copy(out=dst, in_=src)
         quantize(nc, w1_codes[:], w1_scales[:], w1_bf[:])
 
-        parent_last = held.tile([P, 128], F32, name="parent_last", tag="rows", align_bytes=64)
-        nc.vector.tensor_copy(parent_last[:], t_sb[:].indirect(par_sb[:, 56:64]))
-        for a, b in ((0, 448), (448, 896)):
+        for a, b in ((0, 384), (384, 768), (768, 1024)):
             nc.scalar.activation(out=parent[:, a:b], in_=t_sb[:].indirect(par_sb[:, a // PER_COL : b // PER_COL]), func=ACT.Copy)
 
         total = held.tile([P, S], F32, name="total")
@@ -130,7 +128,7 @@ def tile_picked_fpn_relu_p_kernel(tc, x_words, x_scales, sT, w1, w2, offs, par, 
                 y_at.append((bank, a, b))
 
         for bank, c, d in y_at:
-            nc.vector.tensor_tensor(total[:, c:d], bank[:], parent[:, c:d] if d <= 896 else parent_last[:], ALU.add)
+            nc.vector.tensor_tensor(total[:, c:d], bank[:], parent[:, c:d], ALU.add)
             if d == S:
                 nc.vector.tensor_scalar_max(result[:, c:d], total[:, c:d], 0.0)
             else:

@@ -117,7 +117,10 @@ def tile_picked_fpn_relu_p_kernel(tc, x_words, x_scales, sT, w1, w2, offs, par, 
         for g in range(4):
             a0 = g * PIECE
             kept = (kept_early, kept_late)[g // 2][:, a0 % HALF_S : a0 % HALF_S + PIECE]
-            nc.vector.tensor_copy(kept, xw[:].bitcast(U32).indirect(offs_sb[:, a0 // PER_COL : (a0 + PIECE) // PER_COL]))
+            if g == 0:
+                nc.vector.tensor_copy(kept_early[:], xw[:].bitcast(U32).indirect(offs_sb[:, 0 : HALF_S // PER_COL]))
+            if g >= 2:
+                nc.vector.tensor_copy(kept, xw[:].bitcast(U32).indirect(offs_sb[:, a0 // PER_COL : (a0 + PIECE) // PER_COL]))
             for a, b, tag in Y_PASSES[g]:
                 bank = psum.tile([P, b - a], F32, name=f"y_ps{a}", tag=tag)
                 nc.tensor.matmul_mx(
@@ -125,7 +128,7 @@ def tile_picked_fpn_relu_p_kernel(tc, x_words, x_scales, sT, w1, w2, offs, par, 
                     rhs=kept[:, a - a0 : b - a0].bitcast(FP8X4),
                     rhs_scale=kept_scales[:, a:b], start=True, stop=True,
                 )
-                y_at.append((bank, a, b))
+                y_at.extend((bank[:, c - a : c - a + 128], c, c + 128) for c in range(a, b, 128))
 
         for bank, c, d in y_at:
             nc.vector.tensor_tensor(total[:, c:d], bank[:], parent[:, c:d], ALU.add)

@@ -24,7 +24,9 @@ PIECE = 256
 T_PIECES = ((0, 128), (128, 256), (256, 384), (384, 512))
 WEAVES = ((0, 128, True), (256, 384, False), (128, 256, True), (384, 448, False), (448, 512, True))
 ROW0 = 32
-Y_PASSES = (((0, 256, "y0"),), ((256, 512, "y1"),), ((512, 768, "y2"),), ((768, 896, "t0"), (896, 1024, "t128")))
+EARLY = 640
+GATHERS = ((0, EARLY), (EARLY, S))
+Y_PASSES = (((0, 128, "y0"), (128, 384, "y1"), (384, 640, "y2")), ((640, 768, "y3"), (768, 896, "t0"), (896, 1024, "t128")))
 
 
 def weave_views(grouped, raw):
@@ -112,15 +114,9 @@ def tile_picked_fpn_relu_p_kernel(tc, x_words, x_scales, sT, w1, w2, offs, par, 
         total = held.tile([P, S], F32, name="total")
         result = held.tile([P, S], F32, name="result")
         y_at = []
-        kept_late = held.tile([P, HALF_S], U32, name="kept_late", tag="shared", align_bytes=64)
-        kept_early = held.tile([P, HALF_S], U32, name="kept_early", align_bytes=64)
-        for g in range(4):
-            a0 = g * PIECE
-            kept = (kept_early, kept_late)[g // 2][:, a0 % HALF_S : a0 % HALF_S + PIECE]
-            if g == 0:
-                nc.vector.tensor_copy(kept_early[:], xw[:].bitcast(U32).indirect(offs_sb[:, 0 : HALF_S // PER_COL]))
-            if g >= 2:
-                nc.vector.tensor_copy(kept, xw[:].bitcast(U32).indirect(offs_sb[:, a0 // PER_COL : (a0 + PIECE) // PER_COL]))
+        for g, (a0, b0) in enumerate(GATHERS):
+            kept = held.tile([P, b0 - a0], U32, name=f"kept{g}", tag="shared" if g else "early", align_bytes=64)
+            nc.vector.tensor_copy(kept[:], xw[:].bitcast(U32).indirect(offs_sb[:, a0 // PER_COL : b0 // PER_COL]))
             for a, b, tag in Y_PASSES[g]:
                 bank = psum.tile([P, b - a], F32, name=f"y_ps{a}", tag=tag)
                 nc.tensor.matmul_mx(

@@ -26,7 +26,10 @@ WEAVES = ((0, 128, True), (256, 384, False), (128, 256, True), (384, 448, False)
 ROW0 = 32
 EARLY = 640
 GATHERS = ((0, EARLY), (EARLY, S))
-Y_PASSES = (((0, 128, "y0"), (128, 384, "y1"), (384, 640, "y2")), ((640, 768, "y3"), (768, 896, "t0"), (896, 1024, "t128")))
+Y_PASSES = (
+    ((0, 128, "y0"), (128, 256, "y1"), (256, 384, "y2"), (384, 512, "y3"), (512, 640, "t0")),
+    ((640, 768, "t128"), (768, 896, "t256"), (896, 1024, "t384")),
+)
 
 
 def weave_views(grouped, raw):

@@ -52,11 +52,11 @@ def tile_picked_fpn_relu_p_kernel(tc, x_words, x_scales, sT, w1, w2, offs, par, 
 
         offs_sb = lists.tile([P, S // PER_COL], U16, name="offs_sb")
         par_sb = lists.tile([P, S // PER_COL], U16, name="par_sb")
-        xw = held.tile([P, T], I32, name="xw", align_bytes=64)
-        xs = held.tile([P, T], U8, name="xs", align_bytes=64)
-        w1_raw = held.tile([P, PACK, N], F32, name="w1_raw", tag="shared", align_bytes=64)
-        w2_raw = held.tile([P, PACK, N], F32, name="w2_raw")
-        s_raw = held.tile([P, PACK, V], F32, name="s_raw")
+        xw = held.tile([P, T], I32, name="xw", align_bytes=256)
+        xs = held.tile([P, T], U8, name="xs", align_bytes=256)
+        w1_raw = held.tile([P, PACK, N], F32, name="w1_raw", tag="shared", align_bytes=256)
+        w2_raw = held.tile([P, PACK, N], F32, name="w2_raw", align_bytes=256)
+        s_raw = held.tile([P, PACK, V], F32, name="s_raw", align_bytes=256)
 
         nc.vector.memset(xs[:].bitcast(I32), 0)
         s_rows = sT.rearrange("(p j) v -> p j v", j=PACK)
@@ -115,10 +115,10 @@ def tile_picked_fpn_relu_p_kernel(tc, x_words, x_scales, sT, w1, w2, offs, par, 
             nc.scalar.activation(out=parent[:, a:b], in_=t_sb[:].indirect(par_sb[:, a // PER_COL : b // PER_COL]), func=ACT.Copy)
 
         total = held.tile([P, S], F32, name="total")
-        result = held.tile([P, S], F32, name="result")
+        result = held.tile([P, S], F32, name="result", align_bytes=256)
         y_at = []
         for g, (a0, b0) in enumerate(GATHERS):
-            kept = held.tile([P, b0 - a0], U32, name=f"kept{g}", tag="shared" if g else "early", align_bytes=64)
+            kept = held.tile([P, b0 - a0], U32, name=f"kept{g}", tag="shared" if g else "early", align_bytes=256)
             nc.vector.tensor_copy(kept[:], xw[:].bitcast(U32).indirect(offs_sb[:, a0 // PER_COL : b0 // PER_COL]))
             for a, b, tag in Y_PASSES[g]:
                 bank = psum.tile([P, b - a], F32, name=f"y_ps{a}", tag=tag)

@@ -107,9 +107,11 @@ def tile_picked_fpn_relu_p_kernel(tc, x_words, x_scales, sT, w1, w2, offs, par, 
                 out=kept_scales[32 * q : 32 * q + 4, :].bitcast(I32),
                 in_=kept_rows[ROW0 + 16 * q : ROW0 + 16 * q + 16 : 4, :].bitcast(I32),
             )
-        dst, src = weave_views(w1_bf[:], w1_raw[:])
-        nc.scalar.copy(out=dst, in_=src)
-        quantize(nc, w1_codes[:], w1_scales[:], w1_bf[:])
+        for a in range(0, N, N // 2):
+            b = a + N // 2
+            dst, src = weave_views(w1_bf[:, a:b, :], w1_raw[:, :, a:b])
+            nc.scalar.copy(out=dst, in_=src)
+            quantize(nc, w1_codes[:, a:b], w1_scales[:, a:b], w1_bf[:, a:b, :])
 
         for a, b in ((0, 384), (384, 768), (768, 1024)):
             nc.scalar.activation(out=parent[:, a:b], in_=t_sb[:].indirect(par_sb[:, a // PER_COL : b // PER_COL]), func=ACT.Copy)

@@ -20,7 +20,7 @@ PACK = 4
 PER_COL = 16
 HALF_S = S // 2
 HALF_V = V // 2
-PIECE = 256
+STORES = {128: 0, 384: 128, 640: 384, 1024: 640}
 T_PIECES = ((0, 128), (128, 256), (256, 384), (384, 512))
 WEAVES = ((0, 128, True), (256, 384, False), (128, 256, True), (384, 448, False), (448, 512, True))
 ROW0 = 32
@@ -137,5 +137,5 @@ def tile_picked_fpn_relu_p_kernel(tc, x_words, x_scales, sT, w1, w2, offs, par, 
                 nc.vector.tensor_scalar_max(result[:, c:d], total[:, c:d], 0.0)
             else:
                 nc.scalar.activation(out=result[:, c:d], in_=total[:, c:d], func=ACT.Relu)
-            if d % PIECE == 0:
-                nc.sync.dma_start(out=out[:, d - PIECE : d], in_=result[:, d - PIECE : d])
+            if d in STORES:
+                nc.sync.dma_start(out=out[:, STORES[d] : d], in_=result[:, STORES[d] : d])

from contextlib import ExitStack

import concourse.mybir as mybir

K, T, S, V, N = 512, 4096, 1024, 512, 128
FLOPS = 2 * K * N * (S + V)

F32 = mybir.dt.float32
BF16 = mybir.dt.bfloat16
I32 = mybir.dt.int32
U32 = mybir.dt.uint32
U16 = mybir.dt.uint16
U8 = mybir.dt.uint8
FP8X4 = mybir.dt.float8_e4m3fn_x4
ACT = mybir.ActivationFunctionType
ALU = mybir.AluOpType

P = 128
PACK = 4
PER_COL = 16
HALF_S = S // 2
HALF_V = V // 2
STORES = {128: 0, 384: 128, 640: 384, 1024: 640}
T_PIECES = ((0, 128), (128, 256), (256, 384), (384, 512))
WEAVES = ((0, 128, True), (256, 384, False), (128, 256, True), (384, 448, False), (448, 512, True))
ROW0 = 32
EARLY = 640
GATHERS = ((0, EARLY), (EARLY, S))
Y_PASSES = (
    ((0, 128, "y0"), (128, 256, "y1"), (256, 384, "y2"), (384, 512, "y3"), (512, 640, "t0")),
    ((640, 768, "t128"), (768, 896, "t256"), (896, 1024, "t384")),
)


def weave_views(grouped, raw):
    return (
        grouped.rearrange("p (c i) j -> p c j i", i=4),
        raw.rearrange("p j (c i) -> p c j i", i=4),
    )


def quantize(nc, codes, scales, grouped):
    nc.vector.quantize_mx(out=codes.bitcast(FP8X4), scales=scales, in_=grouped.rearrange("p c j -> p (c j)"))


def tile_picked_fpn_relu_p_kernel(tc, x_words, x_scales, sT, w1, w2, offs, par, out):
    nc = tc.nc
    with ExitStack() as ctx:
        lists = ctx.enter_context(tc.tile_pool(name="lists", bufs=1))
        held = ctx.enter_context(tc.tile_pool(name="held", bufs=1))
        psum = ctx.enter_context(tc.psum_pool(name="psum", bufs=1))

        offs_sb = lists.tile([P, S // PER_COL], U16, name="offs_sb")
        par_sb = lists.tile([P, S // PER_COL], U16, name="par_sb")
        xw = held.tile([P, T], I32, name="xw", align_bytes=256)
        xs = held.tile([P, T], U8, name="xs", align_bytes=256)
        w1_raw = held.tile([P, PACK, N], F32, name="w1_raw", tag="shared", align_bytes=256)
        w2_raw = held.tile([P, PACK, N], F32, name="w2_raw", align_bytes=256)
        s_raw = held.tile([P, PACK, V], F32, name="s_raw", align_bytes=256)

        nc.vector.memset(xs[:].bitcast(I32), 0)
        s_rows = sT.rearrange("(p j) v -> p j v", j=PACK)
        nc.sync.dma_start(out=w2_raw[:], in_=w2.rearrange("(p j) n -> p j n", j=PACK))
        nc.sync.dma_start(out=s_raw[:], in_=s_rows)
        nc.sync.dma_start(offs_sb[:], offs)
        nc.sync.dma_start(par_sb[:], par)
        nc.sync.dma_start(out=xs[ROW0 : ROW0 + 64 : 4, :].bitcast(I32), in_=x_scales[0].bitcast(I32))
        nc.sync.dma_start(out=xw[:], in_=x_words[0].rearrange("p c r -> p (c r)").bitcast(I32))
        nc.sync.dma_start(out=w1_raw[:], in_=w1.rearrange("(p j) n -> p j n", j=PACK))

        w1_bf = held.tile([P, N, PACK], BF16, name="w1_bf", align_bytes=64)
        w2_bf = held.tile([P, N, PACK], BF16, name="w2_bf", align_bytes=64)
        s_bf = held.tile([P, V, PACK], BF16, name="s_bf", tag="woven", align_bytes=64)
        w1_codes = held.tile([P, N], U32, name="w1_codes", align_bytes=64)
        w1_scales = held.tile([P, N], U8, name="w1_scales", align_bytes=64)
        w2_codes = held.tile([P, N], U32, name="w2_codes", align_bytes=64)
        w2_scales = held.tile([P, N], U8, name="w2_scales", align_bytes=64)
        s_codes = held.tile([P, V], U32, name="s_codes", align_bytes=64)
        s_scales = held.tile([P, V], U8, name="s_scales", align_bytes=64)
        t_sb = held.tile([P, V], F32, name="t_sb", align_bytes=64)
        parent = held.tile([P, S], F32, name="parent", align_bytes=64)
        t_ps = [psum.tile([P, b - a], F32, name=f"t_ps{a}", tag=f"t{a}") for a, b in T_PIECES]

        dst, src = weave_views(w2_bf[:], w2_raw[:])
        nc.scalar.activation(out=dst, in_=src, func=ACT.Copy)
        quantize(nc, w2_codes[:], w2_scales[:], w2_bf[:])
        for a, b, on_vector in WEAVES:
            dst, src = weave_views(s_bf[:, a:b, :], s_raw[:, :, a:b])
            if on_vector:
                nc.vector.tensor_copy(out=dst, in_=src)
            else:
                nc.scalar.copy(out=dst, in_=src)
        for (a, b), bank in zip(T_PIECES, t_ps):
            quantize(nc, s_codes[:, a:b], s_scales[:, a:b], s_bf[:, a:b, :])
            nc.tensor.matmul_mx(
                out=bank[:], lhsT=w2_codes[:].bitcast(FP8X4), lhsT_scale=w2_scales[:],
                rhs=s_codes[:, a:b].bitcast(FP8X4), rhs_scale=s_scales[:, a:b], start=True, stop=True,
            )
        kept_rows = held.tile([P, S], U8, name="kept_rows", tag="woven", align_bytes=64)
        nc.vector.tensor_copy(kept_rows[:], xs[:].indirect(offs_sb[:]))
        for (a, b), bank in zip(T_PIECES, t_ps):
            nc.scalar.copy(out=t_sb[:, a:b], in_=bank[:])
        kept_scales = held.tile([P, S], U8, name="kept_scales", align_bytes=64)
        nc.vector.memset(kept_scales[:].bitcast(I32), 0)
        for q in range(4):
            nc.sync.dma_start(
                out=kept_scales[32 * q : 32 * q + 4, :].bitcast(I32),
                in_=kept_rows[ROW0 + 16 * q : ROW0 + 16 * q + 16 : 4, :].bitcast(I32),
            )
        for a in range(0, N, N // 2):
            b = a + N // 2
            dst, src = weave_views(w1_bf[:, a:b, :], w1_raw[:, :, a:b])
            nc.scalar.copy(out=dst, in_=src)
            quantize(nc, w1_codes[:, a:b], w1_scales[:, a:b], w1_bf[:, a:b, :])

        for a, b in ((0, 384), (384, 768), (768, 1024)):
            nc.scalar.activation(out=parent[:, a:b], in_=t_sb[:].indirect(par_sb[:, a // PER_COL : b // PER_COL]), func=ACT.Copy)

        total = held.tile([P, S], F32, name="total")
        result = held.tile([P, S], F32, name="result", align_bytes=256)
        y_at = []
        for g, (a0, b0) in enumerate(GATHERS):
            kept = held.tile([P, b0 - a0], U32, name=f"kept{g}", tag="shared" if g else "early", align_bytes=256)
            nc.vector.tensor_copy(kept[:], xw[:].bitcast(U32).indirect(offs_sb[:, a0 // PER_COL : b0 // PER_COL]))
            for a, b, tag in Y_PASSES[g]:
                bank = psum.tile([P, b - a], F32, name=f"y_ps{a}", tag=tag)
                nc.tensor.matmul_mx(
                    out=bank[:], lhsT=w1_codes[:].bitcast(FP8X4), lhsT_scale=w1_scales[:],
                    rhs=kept[:, a - a0 : b - a0].bitcast(FP8X4),
                    rhs_scale=kept_scales[:, a:b], start=True, stop=True,
                )
                y_at.extend((bank[:, c - a : c - a + 128], c, c + 128) for c in range(a, b, 128))

        for bank, c, d in y_at:
            nc.vector.tensor_tensor(total[:, c:d], bank[:], parent[:, c:d], ALU.add)
            if d == S:
                nc.vector.tensor_scalar_max(result[:, c:d], total[:, c:d], 0.0)
            else:
                nc.scalar.activation(out=result[:, c:d], in_=total[:, c:d], func=ACT.Relu)
            if d in STORES:
                nc.sync.dma_start(out=out[:, STORES[d] : d], in_=result[:, STORES[d] : d])
